import numpy as np
import ml_dtypes

BF16 = ml_dtypes.bfloat16


def bf(x):
    return np.asarray(x, np.float32).astype(BF16)


def f32(x):
    return np.asarray(x, np.float32)


def f64(x):
    return np.asarray(x).astype(np.float64)


def striped(idx):
    return np.concatenate([l.reshape(-1, 16).T for l in idx])


def rows(idx, k):
    return np.tile(np.repeat(idx, 16, axis=0), (k // (16 * 8), 1))


def look(tab, idx):
    return np.take_along_axis(f64(tab), rows(idx, len(tab)), axis=1)


K, S, D, V, N, M = 256, 2048, 2, 512, 1024, 256


def setup_inputs():
    return {"tab": f32(np.random.standard_normal((K, S))), "x0": f32(1.0 * np.random.standard_normal((K, V))), "w": bf(np.random.standard_normal((K, M)) / np.sqrt(K)), "b": f32(0.5 * np.random.standard_normal((M, 1))), "offs": striped(np.stack([np.random.permutation(S)[:N] for _ in range(8)]))}


def reference(tab, x0, w, b, offs):
    idx = np.stack([g.T.reshape(-1) for g in np.split(offs, 8)])
    a = (f64(x0) + sum(look(tab, idx[:, d * V:(d + 1) * V]) for d in range(D))) / (D + 1)
    x = ((f64(x0) - a) ** 2 + sum((look(tab, idx[:, d * V:(d + 1) * V]) - a) ** 2 for d in range(D))) / (D + 1)
    return np.maximum(f64(w).T @ x + f64(b), 0.0)

@@ -1,0 +1,87 @@
+import math
+
+import concourse.mybir as mybir
+
+F32, BF16, U16 = mybir.dt.float32, mybir.dt.bfloat16, mybir.dt.uint16
+ADD, SUB, MAX = mybir.AluOpType.add, mybir.AluOpType.subtract, mybir.AluOpType.max
+COPY = mybir.ActivationFunctionType.Copy
+SQUARE = mybir.ActivationFunctionType.Square
+RELU = mybir.ActivationFunctionType.Relu
+
+P = 128
+K, S, D, V, M = 256, 2048, 2, 512, 256
+BLOCKS = K // P
+LIST_COLUMNS = V // 16
+
+FLOPS = 2 * K * M * V
+
+
+def tile_lookup_vari_relu_kernel(tc, tab, x0, w, b, offs, out):
+    nc = tc.nc
+    with (
+        tc.tile_pool(name="held", bufs=1) as held,
+        tc.psum_pool(name="psum", bufs=1) as psum,
+    ):
+        offsets = held.tile([P, D * LIST_COLUMNS], U16, name="offsets")
+        nc.sync.dma_start(offsets[:], offs)
+
+        tables, nodes = [], []
+        for k in range(BLOCKS):
+            rows = slice(k * P, (k + 1) * P)
+            node = held.tile([P, V], F32, name=f"node{k}")
+            table = held.tile([P, S], F32, name=f"table{k}")
+            nc.scalar.dma_start(node[:], x0[rows, :])
+            nc.sync.dma_start(table[:], tab[rows, :])
+            nodes.append(node)
+            tables.append(table)
+        weights = held.tile([P, BLOCKS, M], BF16, name="weights")
+        nc.sync.dma_start(weights[:], w.rearrange("(k p) m -> p k m", p=P))
+        biases = []
+        for m in range(M // P):
+            bias = held.tile([P, 1], F32, name=f"bias{m}")
+            nc.sync.dma_start(bias[:], b[m * P : (m + 1) * P, :])
+            biases.append(bias)
+
+        banks = [psum.tile([P, V], F32, name=f"bank{m}") for m in range(M // P)]
+        variances = []
+        for k in range(BLOCKS):
+            def picked(d):
+                return tables[k][:].indirect(offsets[:, d * LIST_COLUMNS : (d + 1) * LIST_COLUMNS])
+
+            total = nodes[k]
+            for d in range(D):
+                grown = held.tile([P, V], F32, name=f"total{k}_{d}")
+                nc.vector.tensor_tensor(grown[:], picked(d), total[:], ADD)
+                total = grown
+            mean = held.tile([P, V], F32, name=f"mean{k}")
+            nc.scalar.activation(mean[:], total[:], COPY, scale=1.0 / (D + 1))
+
+            squares = []
+            for d in range(-1, D):
+                difference = held.tile([P, V], F32, name=f"difference{k}_{d + 1}")
+                if d < 0:
+                    nc.vector.tensor_tensor(difference[:], nodes[k][:], mean[:], SUB)
+                else:
+                    nc.vector.tensor_tensor(difference[:], picked(d), mean[:], SUB)
+                square = held.tile([P, V], F32, name=f"square{k}_{d + 1}")
+                nc.scalar.activation(square[:], difference[:], SQUARE, scale=1.0 / math.sqrt(D + 1))
+                squares.append(square)
+
+            partial = held.tile([P, V], F32, name=f"partial{k}")
+            nc.vector.tensor_tensor(partial[:], squares[0][:], squares[1][:], ADD)
+            variance = held.tile([P, V], BF16, name=f"variance{k}")
+            nc.vector.tensor_tensor(variance[:], partial[:], squares[2][:], ADD)
+            variances.append(variance)
+
+        for m in range(M // P):
+            columns = slice(m * P, (m + 1) * P)
+            for k in range(BLOCKS):
+                nc.tensor.matmul(banks[m][:], weights[:, k, columns], variances[k][:],
+                                 start=(k == 0), stop=(k == BLOCKS - 1))
+            result = held.tile([P, V], F32, name=f"result{m}")
+            if m % 2 == 0:
+                nc.scalar.activation(result[:], banks[m][:], RELU, bias=biases[m][:])
+                nc.scalar.dma_start(out[columns, :], result[:])
+            else:
+                nc.vector.tensor_scalar(result[:], banks[m][:], biases[m][:], 0.0, ADD, MAX)
+                nc.sync.dma_start(out[columns, :], result[:])

@@ -1,9 +1,11 @@
 import math
 
 import concourse.mybir as mybir
+from concourse.masks import make_identity
 
 F32, BF16, U16 = mybir.dt.float32, mybir.dt.bfloat16, mybir.dt.uint16
-ADD, SUB, MAX = mybir.AluOpType.add, mybir.AluOpType.subtract, mybir.AluOpType.max
+ADD, SUB, MULT, MAX = (mybir.AluOpType.add, mybir.AluOpType.subtract, mybir.AluOpType.mult,
+                       mybir.AluOpType.max)
 COPY = mybir.ActivationFunctionType.Copy
 SQUARE = mybir.ActivationFunctionType.Square
 RELU = mybir.ActivationFunctionType.Relu
@@ -24,13 +26,12 @@ def tile_lookup_vari_relu_kernel(tc, tab, x0, w, b, offs, out):
     ):
         offsets = held.tile([P, D * LIST_COLUMNS], U16, name="offsets")
         nc.sync.dma_start(offsets[:], offs)
-
         tables, nodes = [], []
         for k in range(BLOCKS):
             rows = slice(k * P, (k + 1) * P)
             node = held.tile([P, V], F32, name=f"node{k}")
             table = held.tile([P, S], F32, name=f"table{k}")
-            nc.scalar.dma_start(node[:], x0[rows, :])
+            nc.sync.dma_start(node[:], x0[rows, :])
             nc.sync.dma_start(table[:], tab[rows, :])
             nodes.append(node)
             tables.append(table)
@@ -42,46 +43,86 @@ def tile_lookup_vari_relu_kernel(tc, tab, x0, w, b, offs, out):
             nc.sync.dma_start(bias[:], b[m * P : (m + 1) * P, :])
             biases.append(bias)
 
-        banks = [psum.tile([P, V], F32, name=f"bank{m}") for m in range(M // P)]
-        variances = []
-        for k in range(BLOCKS):
-            def picked(d):
-                return tables[k][:].indirect(offsets[:, d * LIST_COLUMNS : (d + 1) * LIST_COLUMNS])
+        identity = held.tile([P, P], F32, name="identity")
+        make_identity(nc, identity[:])
+        negated = held.tile([P, P], F32, name="negated")
+        nc.scalar.activation(negated[:], identity[:], COPY, scale=-1.0)
 
-            total = nodes[k]
-            for d in range(D):
-                grown = held.tile([P, V], F32, name=f"total{k}_{d}")
-                nc.vector.tensor_tensor(grown[:], picked(d), total[:], ADD)
-                total = grown
+        def picked(k, d):
+            return tables[k][:].indirect(offsets[:, d * LIST_COLUMNS : (d + 1) * LIST_COLUMNS])
+
+        def add_neighbour(k, d, running):
+            grown = held.tile([P, V], F32, name=f"total{k}_{d}")
+            nc.vector.tensor_tensor(grown[:], picked(k, d), running[:], ADD)
+            return grown
+
+        def mean_of(k, total):
             mean = held.tile([P, V], F32, name=f"mean{k}")
             nc.scalar.activation(mean[:], total[:], COPY, scale=1.0 / (D + 1))
+            return mean
 
-            squares = []
-            for d in range(-1, D):
-                difference = held.tile([P, V], F32, name=f"difference{k}_{d + 1}")
-                if d < 0:
-                    nc.vector.tensor_tensor(difference[:], nodes[k][:], mean[:], SUB)
+        def difference_of(k, d, mean):
+            difference = held.tile([P, V], F32, name=f"difference{k}_{d}")
+            nc.vector.tensor_tensor(difference[:], picked(k, d), mean[:], SUB)
+            return difference
+
+        def node_difference_of(k, mean):
+            difference = psum.tile([P, V], F32, name=f"node_difference{k}")
+            nc.tensor.matmul(difference[:], identity[:], nodes[k][:], start=True, stop=False)
+            nc.tensor.matmul(difference[:], negated[:], mean[:], start=False, stop=True)
+            return difference
+
+        def square_of(name, difference):
+            square = held.tile([P, V], F32, name=f"square_{name}")
+            nc.scalar.activation(square[:], difference[:], SQUARE, scale=1.0 / math.sqrt(D + 1))
+            return square
+
+        def sum_of(name, dtype, left, right):
+            total = held.tile([P, V], dtype, name=name)
+            nc.vector.tensor_tensor(total[:], left[:], right[:], ADD)
+            return total
+
+        total0 = add_neighbour(0, 1, add_neighbour(0, 0, nodes[0]))
+        mean0 = mean_of(0, total0)
+        running1 = add_neighbour(1, 0, nodes[1])
+        node0 = square_of("0_node", node_difference_of(0, mean0))
+        near0 = square_of("0_0", difference_of(0, 0, mean0))
+        mean1 = mean_of(1, add_neighbour(1, 1, running1))
+        far0 = square_of("0_1", difference_of(0, 1, mean0))
+        near1 = square_of("1_0", difference_of(1, 0, mean1))
+        node1 = square_of("1_node", node_difference_of(1, mean1))
+        variance0 = sum_of("variance0", BF16, sum_of("partial0", F32, node0, near0), far0)
+        partial1 = sum_of("partial1", F32, near1, node1)
+
+        H = V // 2
+        banks = {}
+        for h in range(2):
+            for m in range(M // P):
+                bank = psum.tile([P, H], F32, name=f"bank{h}_{m}")
+                nc.tensor.matmul(bank[:], weights[:, 0, m * P : (m + 1) * P], variance0[:, h * H : (h + 1) * H],
+                                 start=True, stop=False)
+                banks[h, m] = bank
+
+        difference1 = difference_of(1, 1, mean1)
+        first_square = held.tile([P, H], F32, name="first_square")
+        nc.scalar.activation(first_square[:], difference1[:, :H], SQUARE, scale=1.0 / math.sqrt(D + 1))
+        second_square = held.tile([P, H], F32, name="second_square")
+        nc.vector.scalar_tensor_tensor(second_square[:], difference1[:, H:], 1.0 / (D + 1), difference1[:, H:], MULT, MULT)
+        halves = []
+        for h, square in enumerate((first_square, second_square)):
+            half = held.tile([P, H], BF16, name=f"variance1_{h}")
+            nc.vector.tensor_tensor(half[:], partial1[:, h * H : (h + 1) * H], square[:], ADD)
+            halves.append(half)
+
+        for h in range(2):
+            columns = slice(h * H, (h + 1) * H)
+            for m in range(M // P):
+                rows = slice(m * P, (m + 1) * P)
+                nc.tensor.matmul(banks[h, m][:], weights[:, 1, rows], halves[h][:], start=False, stop=True)
+                result = held.tile([P, H], F32, name=f"result{h}_{m}")
+                if m == 0:
+                    nc.scalar.activation(result[:], banks[h, m][:], RELU, bias=biases[m][:])
+                    nc.scalar.dma_start(out[rows, columns], result[:])
                 else:
-                    nc.vector.tensor_tensor(difference[:], picked(d), mean[:], SUB)
-                square = held.tile([P, V], F32, name=f"square{k}_{d + 1}")
-                nc.scalar.activation(square[:], difference[:], SQUARE, scale=1.0 / math.sqrt(D + 1))
-                squares.append(square)
-
-            partial = held.tile([P, V], F32, name=f"partial{k}")
-            nc.vector.tensor_tensor(partial[:], squares[0][:], squares[1][:], ADD)
-            variance = held.tile([P, V], BF16, name=f"variance{k}")
-            nc.vector.tensor_tensor(variance[:], partial[:], squares[2][:], ADD)
-            variances.append(variance)
-
-        for m in range(M // P):
-            columns = slice(m * P, (m + 1) * P)
-            for k in range(BLOCKS):
-                nc.tensor.matmul(banks[m][:], weights[:, k, columns], variances[k][:],
-                                 start=(k == 0), stop=(k == BLOCKS - 1))
-            result = held.tile([P, V], F32, name=f"result{m}")
-            if m % 2 == 0:
-                nc.scalar.activation(result[:], banks[m][:], RELU, bias=biases[m][:])
-                nc.scalar.dma_start(out[columns, :], result[:])
-            else:
-                nc.vector.tensor_scalar(result[:], banks[m][:], biases[m][:], 0.0, ADD, MAX)
-                nc.sync.dma_start(out[columns, :], result[:])
+                    nc.vector.tensor_scalar(result[:], banks[h, m][:], biases[m][:], 0.0, ADD, MAX)
+                    nc.sync.dma_start(out[rows, columns], result[:])

@@ -91,8 +91,10 @@ def tile_lookup_vari_relu_kernel(tc, tab, x0, w, b, offs, out):
         far0 = square_of("0_1", difference_of(0, 1, mean0))
         near1 = square_of("1_0", difference_of(1, 0, mean1))
         node1 = square_of("1_node", node_difference_of(1, mean1))
-        variance0 = sum_of("variance0", BF16, sum_of("partial0", F32, node0, near0), far0)
+        partial0 = sum_of("partial0", F32, node0, near0)
+        difference1 = difference_of(1, 1, mean1)
         partial1 = sum_of("partial1", F32, near1, node1)
+        variance0 = sum_of("variance0", BF16, partial0, far0)
 
         H = V // 2
         banks = {}
@@ -103,15 +105,15 @@ def tile_lookup_vari_relu_kernel(tc, tab, x0, w, b, offs, out):
                                  start=True, stop=False)
                 banks[h, m] = bank
 
-        difference1 = difference_of(1, 1, mean1)
-        first_square = held.tile([P, H], F32, name="first_square")
-        nc.scalar.activation(first_square[:], difference1[:, :H], SQUARE, scale=1.0 / math.sqrt(D + 1))
-        second_square = held.tile([P, H], F32, name="second_square")
-        nc.vector.scalar_tensor_tensor(second_square[:], difference1[:, H:], 1.0 / (D + 1), difference1[:, H:], MULT, MULT)
+        last_squares = []
+        for h in range(2):
+            square = held.tile([P, H], F32, name=f"last_square{h}")
+            nc.scalar.activation(square[:], difference1[:, h * H : (h + 1) * H], SQUARE, scale=1.0 / math.sqrt(D + 1))
+            last_squares.append(square)
         halves = []
-        for h, square in enumerate((first_square, second_square)):
+        for h in range(2):
             half = held.tile([P, H], BF16, name=f"variance1_{h}")
-            nc.vector.tensor_tensor(half[:], partial1[:, h * H : (h + 1) * H], square[:], ADD)
+            nc.vector.tensor_tensor(half[:], partial1[:, h * H : (h + 1) * H], last_squares[h][:], ADD)
             halves.append(half)
 
         for h in range(2):
@@ -122,7 +124,6 @@ def tile_lookup_vari_relu_kernel(tc, tab, x0, w, b, offs, out):
                 result = held.tile([P, H], F32, name=f"result{h}_{m}")
                 if m == 0:
                     nc.scalar.activation(result[:], banks[h, m][:], RELU, bias=biases[m][:])
-                    nc.scalar.dma_start(out[rows, columns], result[:])
                 else:
                     nc.vector.tensor_scalar(result[:], banks[h, m][:], biases[m][:], 0.0, ADD, MAX)
-                    nc.sync.dma_start(out[rows, columns], result[:])
+                nc.sync.dma_start(out[rows, columns], result[:])

import math

import concourse.mybir as mybir
from concourse.masks import make_identity

F32, BF16, U16 = mybir.dt.float32, mybir.dt.bfloat16, mybir.dt.uint16
ADD, SUB, MULT, MAX = (mybir.AluOpType.add, mybir.AluOpType.subtract, mybir.AluOpType.mult,
                       mybir.AluOpType.max)
COPY = mybir.ActivationFunctionType.Copy
SQUARE = mybir.ActivationFunctionType.Square
RELU = mybir.ActivationFunctionType.Relu

P = 128
K, S, D, V, M = 256, 2048, 2, 512, 256
BLOCKS = K // P
LIST_COLUMNS = V // 16

FLOPS = 2 * K * M * V


def tile_lookup_vari_relu_kernel(tc, tab, x0, w, b, offs, out):
    nc = tc.nc
    with (
        tc.tile_pool(name="held", bufs=1) as held,
        tc.psum_pool(name="psum", bufs=1) as psum,
    ):
        offsets = held.tile([P, D * LIST_COLUMNS], U16, name="offsets")
        nc.sync.dma_start(offsets[:], offs)
        tables, nodes = [], []
        for k in range(BLOCKS):
            rows = slice(k * P, (k + 1) * P)
            node = held.tile([P, V], F32, name=f"node{k}")
            table = held.tile([P, S], F32, name=f"table{k}")
            nc.sync.dma_start(node[:], x0[rows, :])
            nc.sync.dma_start(table[:], tab[rows, :])
            nodes.append(node)
            tables.append(table)
        weights = held.tile([P, BLOCKS, M], BF16, name="weights")
        nc.sync.dma_start(weights[:], w.rearrange("(k p) m -> p k m", p=P))
        biases = []
        for m in range(M // P):
            bias = held.tile([P, 1], F32, name=f"bias{m}")
            nc.sync.dma_start(bias[:], b[m * P : (m + 1) * P, :])
            biases.append(bias)

        identity = held.tile([P, P], F32, name="identity")
        make_identity(nc, identity[:])
        negated = held.tile([P, P], F32, name="negated")
        nc.scalar.activation(negated[:], identity[:], COPY, scale=-1.0)

        def picked(k, d):
            return tables[k][:].indirect(offsets[:, d * LIST_COLUMNS : (d + 1) * LIST_COLUMNS])

        def add_neighbour(k, d, running):
            grown = held.tile([P, V], F32, name=f"total{k}_{d}")
            nc.vector.tensor_tensor(grown[:], picked(k, d), running[:], ADD)
            return grown

        def mean_of(k, total):
            mean = held.tile([P, V], F32, name=f"mean{k}")
            nc.scalar.activation(mean[:], total[:], COPY, scale=1.0 / (D + 1))
            return mean

        def difference_of(k, d, mean):
            difference = held.tile([P, V], F32, name=f"difference{k}_{d}")
            nc.vector.tensor_tensor(difference[:], picked(k, d), mean[:], SUB)
            return difference

        def node_difference_of(k, mean):
            difference = psum.tile([P, V], F32, name=f"node_difference{k}")
            nc.tensor.matmul(difference[:], identity[:], nodes[k][:], start=True, stop=False)
            nc.tensor.matmul(difference[:], negated[:], mean[:], start=False, stop=True)
            return difference

        def square_of(name, difference):
            square = held.tile([P, V], F32, name=f"square_{name}")
            nc.scalar.activation(square[:], difference[:], SQUARE, scale=1.0 / math.sqrt(D + 1))
            return square

        def sum_of(name, dtype, left, right):
            total = held.tile([P, V], dtype, name=name)
            nc.vector.tensor_tensor(total[:], left[:], right[:], ADD)
            return total

        total0 = add_neighbour(0, 1, add_neighbour(0, 0, nodes[0]))
        mean0 = mean_of(0, total0)
        running1 = add_neighbour(1, 0, nodes[1])
        node0 = square_of("0_node", node_difference_of(0, mean0))
        near0 = square_of("0_0", difference_of(0, 0, mean0))
        mean1 = mean_of(1, add_neighbour(1, 1, running1))
        far0 = square_of("0_1", difference_of(0, 1, mean0))
        near1 = square_of("1_0", difference_of(1, 0, mean1))
        node1 = square_of("1_node", node_difference_of(1, mean1))
        partial0 = sum_of("partial0", F32, node0, near0)
        difference1 = difference_of(1, 1, mean1)
        partial1 = sum_of("partial1", F32, near1, node1)
        variance0 = sum_of("variance0", BF16, partial0, far0)

        H = V // 2
        banks = {}
        for h in range(2):
            for m in range(M // P):
                bank = psum.tile([P, H], F32, name=f"bank{h}_{m}")
                nc.tensor.matmul(bank[:], weights[:, 0, m * P : (m + 1) * P], variance0[:, h * H : (h + 1) * H],
                                 start=True, stop=False)
                banks[h, m] = bank

        last_squares = []
        for h in range(2):
            square = held.tile([P, H], F32, name=f"last_square{h}")
            nc.scalar.activation(square[:], difference1[:, h * H : (h + 1) * H], SQUARE, scale=1.0 / math.sqrt(D + 1))
            last_squares.append(square)
        halves = []
        for h in range(2):
            half = held.tile([P, H], BF16, name=f"variance1_{h}")
            nc.vector.tensor_tensor(half[:], partial1[:, h * H : (h + 1) * H], last_squares[h][:], ADD)
            halves.append(half)

        for h in range(2):
            columns = slice(h * H, (h + 1) * H)
            for m in range(M // P):
                rows = slice(m * P, (m + 1) * P)
                nc.tensor.matmul(banks[h, m][:], weights[:, 1, rows], halves[h][:], start=False, stop=True)
                result = held.tile([P, H], F32, name=f"result{h}_{m}")
                if m == 0:
                    nc.scalar.activation(result[:], banks[h, m][:], RELU, bias=biases[m][:])
                else:
                    nc.vector.tensor_scalar(result[:], banks[h, m][:], biases[m][:], 0.0, ADD, MAX)
                nc.sync.dma_start(out[rows, columns], result[:])
